import numpy as np
import ml_dtypes


def mxq(x, axis, fmt="e4m3"):
    dtype, down = {"e4m3": (ml_dtypes.float8_e4m3fn, 7), "e5m2": (ml_dtypes.float8_e5m2, 14)}[fmt]
    v = np.moveaxis(np.asarray(x, np.float32).astype(ml_dtypes.bfloat16).astype(np.float64), axis, -1)
    blocks = v.reshape(v.shape[:-1] + (-1, 32))
    amax = np.abs(blocks).max(-1, keepdims=True)
    byte = np.maximum(np.where(amax > 0, np.frexp(amax)[1] - 1 + 127, 0) - down, 1)
    scale = np.exp2(byte - 127.0)
    codes = (blocks / scale).astype(np.float32).astype(dtype).astype(np.float64)
    return np.moveaxis((codes * scale).reshape(v.shape), -1, axis)


WIDE = False


def mx_kscale(k):
    if not WIDE:
        return np.ones(k)
    levels = np.array([10, -10, 5, -5, 0])
    if k % 512:
        return np.exp2(np.random.permutation(np.resize(levels, k // 32))).repeat(32)
    a = np.empty((k // 512, 16))
    for p in range(k // 512):
        a[p, :8] = np.random.permutation(np.resize(levels, 8))
        for g in range(8):
            far = levels[np.abs(levels - a[p, g]) >= 10]
            a[p, g + 8] = far[np.random.randint(len(far))]
    return np.exp2(a.ravel()).repeat(32)


def f64(x):
    return np.asarray(x).astype(np.float64)


def striped(idx):
    return np.tile(idx.reshape(-1, 16).T, (8, 1)).astype(np.uint16)


def unstriped(offs):
    return offs[:16].T.reshape(-1).astype(np.int64)


def striped8(idx):
    return np.concatenate([x.reshape(-1, 16).T for x in idx]).astype(np.uint16)


def runs(offs, k):
    lists = np.stack([offs[16 * r : 16 * r + 16].T.reshape(-1) for r in range(8)]).astype(np.int64)
    return lists[np.arange(k) % 512 // 64]


def pack_weight(w):
    k, n = w.shape
    w = f64(np.asarray(w, np.float32).astype(ml_dtypes.bfloat16)).reshape(k // 32, 32, n)
    amax = np.abs(w).max(1)
    byte = np.clip(np.where(amax > 0, np.frexp(amax)[1] - 1 + 127 - 7, 1), 1, 254)
    scaled = (w * np.exp2(127.0 - byte)[:, None, :]).reshape(k, n).astype(np.float32)
    words = np.ascontiguousarray(scaled.reshape(k // 512, 128, 4, n).transpose(0, 1, 3, 2)).astype(ml_dtypes.float8_e4m3fn).view(np.uint8)
    return words, np.ascontiguousarray(byte.astype(np.uint8).reshape(k // 512, 16, n))


def unpack_weight(words, scales):
    g, p, n, _ = words.shape
    vals = np.ascontiguousarray(words).view(ml_dtypes.float8_e4m3fn).astype(np.float64) * np.repeat(np.exp2(scales.astype(np.float64) - 127.0), 8, axis=1)[..., None]
    return vals.transpose(0, 1, 3, 2).reshape(g * 512, n)


def relu(v):
    return np.maximum(v, 0.0)

def planes(y):
    n, m = y.shape
    v = y.astype(np.float32).astype(ml_dtypes.bfloat16).astype(np.float64).reshape(n // 32, 32, m)
    top = np.abs(v).max(1)
    byte = np.clip(np.where(top > 0, np.frexp(top)[1] - 1 + 127 - 7, 1), 1, 254)
    codes = (v * np.exp2(127.0 - byte)[:, None, :]).reshape(n, m).astype(np.float32).astype(ml_dtypes.float8_e4m3fn).view(np.uint8)
    words = codes.reshape(n // 512, 128, 4, m).transpose(0, 1, 3, 2)
    return np.ascontiguousarray(words), np.ascontiguousarray(byte.astype(np.uint8).reshape(n // 512, 16, m))


K, T, S, G, H, C, U = 512, 1024, 512, 2048, 512, 512, 1024


def setup_inputs():
    n = np.random.standard_normal
    s = mx_kscale(K)[:, None]
    packed_xT = pack_weight(n((K, T)) * s)
    packed_dT = pack_weight(n((K, G)) / s)
    return {
        "x_words": packed_xT[0],
        "x_scales": packed_xT[1],
        "d_words": packed_dT[0],
        "d_scales": packed_dT[1],
        "gs": (np.random.uniform(0.5, 1.5, (K, 1)) / s).astype(np.float32),
        "offs": striped(np.random.permutation(T)[:S]),
        "k1": striped8(np.random.randint(0, G, (8, H))),
        "n1": striped8(np.stack([np.random.permutation(S) for _ in range(8)])),
        "n2": striped8(np.stack([np.random.permutation(S) for _ in range(8)])),
        "cand": striped(np.random.permutation(T)[:C]),
        "n3": striped8(np.stack([np.random.permutation(U)[:S] for _ in range(8)])),
        "n4": striped8(np.stack([np.random.permutation(S) for _ in range(8)])),
    }


def reference(x_words, x_scales, d_words, d_scales, gs, offs, k1, n1, n2, cand, n3, n4):
    x_cand = unpack_weight(x_words, x_scales)[:, unstriped(cand)]
    d_k1 = unpack_weight(d_words, d_scales)[np.arange(K)[:, None], runs(k1, K)]
    xq = unpack_weight(x_words, x_scales)[:, unstriped(offs)]
    h = 0.0625 * (d_k1.T @ xq)
    z = f64(gs) * (np.minimum(np.maximum(h, h[np.arange(H)[:, None], runs(n1, H)]), h[np.arange(H)[:, None], runs(n2, H)]))
    s = 0.0625 * ((x_cand.T @ mxq(z, 0, "e4m3")))
    nw = s - (relu(s[np.arange(C)[:, None], runs(n4, C)]))
    out = np.zeros((C, U))
    out[np.arange(C)[:, None], runs(n3, C)] = nw
    return (out,) + planes(out)

@@ -1,0 +1,208 @@
+from contextlib import ExitStack
+
+import concourse.mybir as mybir
+
+K, T, S, G, H, C, U = 512, 1024, 512, 2048, 512, 512, 1024
+FLOPS = 2 * K * H * S + 2 * K * C * S
+
+F32 = mybir.dt.float32
+BF16 = mybir.dt.bfloat16
+I32 = mybir.dt.int32
+U32 = mybir.dt.uint32
+U16 = mybir.dt.uint16
+U8 = mybir.dt.uint8
+FP8X4 = mybir.dt.float8_e4m3fn_x4
+ALU = mybir.AluOpType
+ACT = mybir.ActivationFunctionType
+
+P = 128
+PACK = 4
+SIXTEENTH = 0.0625
+CHUNK = 256
+CHUNKS = U // CHUNK
+VECTOR_CHUNKS = 2
+
+
+def tile_picked_pqcminmxpagez_none_po_kernel(
+    tc, x_words, x_scales, d_words, d_scales, gs, offs, k1, n1, n2, cand, n3, n4, out_0, out_1, out_2
+):
+    nc = tc.nc
+    with ExitStack() as ctx:
+        lists = ctx.enter_context(tc.tile_pool(name="lists", bufs=1))
+        keep = ctx.enter_context(tc.tile_pool(name="keep", bufs=1))
+        psum = ctx.enter_context(tc.psum_pool(name="psum", bufs=1))
+
+        def load_list(source, name):
+            tile = lists.tile([P, S // 16], U16, name=name)
+            nc.sync.dma_start(tile[:], source)
+            return tile
+
+        def zero_bytes(tile):
+            nc.vector.memset(tile[:].bitcast(I32), 0)
+
+        def place_scale_rows(placed, picked):
+            for c in range(PACK):
+                queue = nc.sync if c % 2 == 0 else nc.scalar
+                queue.dma_start(placed[c:P:32, :].bitcast(I32), picked[8 * c : P : 32, :].bitcast(I32))
+
+        def deal(dealt, picked):
+            nc.vector.tensor_copy(
+                out=dealt.rearrange("p (t m) -> p m t", t=PACK), in_=picked.rearrange("p (m t) -> p m t", t=PACK)
+            )
+
+        x_byte_table = keep.tile([P, T], U8, name="x_byte_table", align_bytes=64)
+        d_byte_table = keep.tile([P, G], U8, name="d_byte_table", tag="d_bytes_then_words", align_bytes=64)
+        zero_bytes(x_byte_table)
+        zero_bytes(d_byte_table)
+
+        offs_list = load_list(offs, "offs_list")
+        k1_list = load_list(k1, "k1_list")
+        nc.scalar.dma_start(x_byte_table[0:P:8, :].bitcast(I32), x_scales[0].bitcast(I32))
+        nc.scalar.dma_start(d_byte_table[0:P:8, :].bitcast(I32), d_scales[0].bitcast(I32))
+        x_word_table = keep.tile([P, T], I32, name="x_word_table", align_bytes=64)
+        nc.sync.dma_start(x_word_table[:], x_words[0].rearrange("p n t -> p (n t)").bitcast(I32))
+        d_word_table = keep.tile([P, G], I32, name="d_word_table", align_bytes=64)
+        nc.sync.dma_start(d_word_table[:], d_words[0].rearrange("p n t -> p (n t)").bitcast(I32))
+        cand_list = load_list(cand, "cand_list")
+        gain = keep.tile([P, PACK], F32, name="gain")
+        nc.gpsimd.dma_start(gain[:], gs.rearrange("(p t) o -> p (t o)", t=PACK))
+        n1_list = load_list(n1, "n1_list")
+        n2_list = load_list(n2, "n2_list")
+        n4_list = load_list(n4, "n4_list")
+        n3_list = load_list(n3, "n3_list")
+
+        first_placed = keep.tile([P, H + S], U8, name="first_placed", align_bytes=64)
+        cand_placed = keep.tile([P, C], U8, name="cand_placed", align_bytes=64)
+        zero_bytes(first_placed)
+        zero_bytes(cand_placed)
+        rows = [keep.tile([P, 2 * S], F32, name="rows%d" % t) for t in range(PACK)]
+        nc.vector.memset(rows[0][:, S:], 0.0)
+        pages = [keep.tile([P, U], F32, name="page%d" % i) for i in range(2)]
+        for page in pages:
+            nc.vector.memset(page[:], 0.0)
+
+        first_picked = keep.tile([P, H + S], U8, name="first_picked", align_bytes=64)
+        nc.vector.tensor_copy(first_picked[:, H:], x_byte_table[:].indirect(offs_list[:]))
+        nc.vector.tensor_copy(first_picked[:, :H], d_byte_table[:].indirect(k1_list[:]))
+        place_scale_rows(first_placed, first_picked)
+        d_picked = keep.tile([P, H], U32, name="d_picked", tag="d_bytes_then_words", align_bytes=64)
+        nc.vector.tensor_copy(d_picked[:], d_word_table[:].bitcast(U32).indirect(k1_list[:]))
+        token_words = keep.tile([P, S], U32, name="token_words", align_bytes=64)
+        nc.vector.tensor_copy(token_words[:], x_word_table[:].bitcast(U32).indirect(offs_list[:]))
+        d_dealt = keep.tile([P, H], U32, name="d_dealt", align_bytes=64)
+        deal(d_dealt[:], d_picked[:])
+        d_scale_dealt = keep.tile([P, H], U8, name="d_scale_dealt", align_bytes=64)
+        deal(d_scale_dealt[:], first_placed[:, :H])
+
+        cand_bytes = keep.tile([P, C], U8, name="cand_bytes", align_bytes=64)
+        nc.vector.tensor_copy(cand_bytes[:], x_byte_table[:].indirect(cand_list[:]))
+        place_scale_rows(cand_placed, cand_bytes)
+
+        for t in range(PACK):
+            cols = slice(t * P, (t + 1) * P)
+            h_bank = psum.tile([P, S], F32, name="h_bank%d" % t)
+            nc.tensor.matmul_mx(
+                out=h_bank[:],
+                lhsT=d_dealt[:, cols].bitcast(FP8X4),
+                lhsT_scale=d_scale_dealt[:, cols],
+                rhs=token_words[:].bitcast(FP8X4),
+                rhs_scale=first_placed[:, H:],
+                start=True,
+                stop=True,
+            )
+            nc.scalar.activation(rows[t][:, :S], h_bank[:], ACT.Copy, scale=SIXTEENTH)
+
+        z_grouped = keep.tile([P, S, PACK], BF16, name="z_grouped", tag="z_then_page", align_bytes=64)
+        last_first = keep.tile([P, S], F32, name="last_first", tag="last_then_cand", align_bytes=64)
+        firsts = [rows[t + 1][:, S:] for t in range(PACK - 1)] + [last_first[:]]
+        seconds = [keep.tile([P, S], F32, name="second%d" % t) for t in range(PACK)]
+        larger = [keep.tile([P, S], F32, name="larger%d" % t) for t in range(PACK)]
+        smaller = [keep.tile([P, S], F32, name="smaller%d" % t) for t in range(PACK)]
+
+        def finish_z(t):
+            nc.vector.tensor_tensor(smaller[t][:], larger[t][:], seconds[t][:], ALU.min)
+            nc.scalar.activation(z_grouped[:, :, t], smaller[t][:], ACT.Copy, scale=gain[:, t : t + 1])
+
+        for t in range(PACK):
+            nc.vector.tensor_copy(firsts[t], rows[t][:].indirect(n1_list[:]))
+            if t > 0:
+                finish_z(t - 1)
+            nc.vector.tensor_copy(seconds[t][:], rows[t][:].indirect(n2_list[:]))
+            nc.vector.tensor_tensor(larger[t][:], rows[t][:, :S], firsts[t], ALU.max)
+        finish_z(PACK - 1)
+
+        cand_picked = keep.tile([P, C], U32, name="cand_picked", tag="last_then_cand", align_bytes=64)
+        nc.vector.tensor_copy(cand_picked[:], x_word_table[:].bitcast(U32).indirect(cand_list[:]))
+        cand_scale_dealt = keep.tile([P, C], U8, name="cand_scale_dealt", align_bytes=64)
+        deal(cand_scale_dealt[:], cand_placed[:])
+        cand_dealt = keep.tile([P, C], U32, name="cand_dealt", align_bytes=64)
+        deal(cand_dealt[:], cand_picked[:])
+
+        z_words = keep.tile([P, S], U32, name="z_words", align_bytes=64)
+        z_scales = keep.tile([P, S], U8, name="z_scales", align_bytes=64)
+        nc.vector.quantize_mx(
+            out=z_words[:].bitcast(FP8X4), scales=z_scales[:], in_=z_grouped[:].rearrange("p s t -> p (s t)")
+        )
+        third_page = keep.tile([P, U], F32, name="page2", tag="z_then_page", align_bytes=64)
+        nc.vector.memset(third_page[:], 0.0)
+        pages.append(third_page)
+
+        s_banks = []
+        scores = [keep.tile([P, S], F32, name="score%d" % t) for t in range(PACK)]
+        for t in range(PACK):
+            cols = slice(t * P, (t + 1) * P)
+            s_bank = psum.tile([P, S], F32, name="s_bank%d" % t)
+            nc.tensor.matmul_mx(
+                out=s_bank[:],
+                lhsT=cand_dealt[:, cols].bitcast(FP8X4),
+                lhsT_scale=cand_scale_dealt[:, cols],
+                rhs=z_words[:].bitcast(FP8X4),
+                rhs_scale=z_scales[:],
+                start=True,
+                stop=True,
+            )
+            s_banks.append(s_bank)
+            nc.scalar.activation(rows[t][:, :S], s_bank[:], ACT.Relu, scale=SIXTEENTH)
+            if t > 0:
+                nc.scalar.activation(scores[t - 1][:], s_banks[t - 1][:], ACT.Copy, scale=SIXTEENTH)
+        nc.scalar.activation(scores[PACK - 1][:], s_banks[PACK - 1][:], ACT.Copy, scale=SIXTEENTH)
+
+        grouped = [keep.tile([P, CHUNK, PACK], BF16, name="grouped%d" % c, align_bytes=64) for c in range(CHUNKS)]
+        out_words = keep.tile([P, U], U32, name="out_words", align_bytes=64)
+        out_scales = keep.tile([P, U], U8, name="out_scales", align_bytes=64)
+        out_rows = out_0.rearrange("(p t) u -> t p u", t=PACK)
+        negated = [keep.tile([P, S], F32, name="negated%d" % t) for t in range(PACK)]
+
+        def look_up(t):
+            nc.vector.tensor_scalar(negated[t][:], rows[t][:].indirect(n4_list[:]), -1.0, 0.0, ALU.mult, ALU.add)
+
+        look_up(0)
+        for t in range(PACK):
+            if t + 1 < PACK:
+                look_up(t + 1)
+            page = pages[t % len(pages)]
+            nc.vector.tensor_tensor(page[:].indirect(n3_list[:]), scores[t][:], negated[t][:], ALU.add)
+            nc.sync.dma_start(out_rows[t], page[:])
+            for c in range(CHUNKS):
+                piece = page[:, c * CHUNK : (c + 1) * CHUNK]
+                if c < VECTOR_CHUNKS and t == PACK - 2:
+                    nc.scalar.copy(grouped[c][:, :, t:], piece.unsqueeze(2).broadcast_to([P, CHUNK, 2]))
+                elif c < VECTOR_CHUNKS and t == PACK - 1:
+                    nc.vector.tensor_copy(grouped[c][:, :, t], piece)
+                else:
+                    nc.scalar.copy(grouped[c][:, :, t], piece)
+
+        out_word_rows = out_1[0].rearrange("p u t -> p (u t)").bitcast(I32)
+        for c in range(CHUNKS):
+            cols = slice(c * CHUNK, (c + 1) * CHUNK)
+            nc.vector.quantize_mx(
+                out=out_words[:, cols].bitcast(FP8X4),
+                scales=out_scales[:, cols],
+                in_=grouped[c][:].rearrange("p u t -> p (u t)"),
+            )
+            if c % 2 == 1:
+                pair = slice((c - 1) * CHUNK, (c + 1) * CHUNK)
+                nc.sync.dma_start(out_word_rows[:, pair], out_words[:, pair].bitcast(I32))
+        for q in range(PACK):
+            queue = nc.scalar if q % 2 == 0 else nc.sync
+            queue.dma_start(out_2[0, 4 * q : 4 * q + 4, :].bitcast(I32), out_scales[32 * q : 32 * q + 4, :].bitcast(I32))

@@ -18,6 +18,7 @@ ACT = mybir.ActivationFunctionType
 P = 128
 PACK = 4
 SIXTEENTH = 0.0625
+HALF = S // 2
 CHUNK = 256
 CHUNKS = U // CHUNK
 VECTOR_CHUNKS = 2
@@ -42,8 +43,7 @@ def tile_picked_pqcminmxpagez_none_po_kernel(
 
         def place_scale_rows(placed, picked):
             for c in range(PACK):
-                queue = nc.sync if c % 2 == 0 else nc.scalar
-                queue.dma_start(placed[c:P:32, :].bitcast(I32), picked[8 * c : P : 32, :].bitcast(I32))
+                nc.sync.dma_start(placed[c:P:32, :].bitcast(I32), picked[8 * c : P : 32, :].bitcast(I32))
 
         def deal(dealt, picked):
             nc.vector.tensor_copy(
@@ -52,20 +52,20 @@ def tile_picked_pqcminmxpagez_none_po_kernel(
 
         x_byte_table = keep.tile([P, T], U8, name="x_byte_table", align_bytes=64)
         d_byte_table = keep.tile([P, G], U8, name="d_byte_table", tag="d_bytes_then_words", align_bytes=64)
-        zero_bytes(x_byte_table)
         zero_bytes(d_byte_table)
+        zero_bytes(x_byte_table)
 
-        offs_list = load_list(offs, "offs_list")
         k1_list = load_list(k1, "k1_list")
-        nc.scalar.dma_start(x_byte_table[0:P:8, :].bitcast(I32), x_scales[0].bitcast(I32))
-        nc.scalar.dma_start(d_byte_table[0:P:8, :].bitcast(I32), d_scales[0].bitcast(I32))
+        offs_list = load_list(offs, "offs_list")
         x_word_table = keep.tile([P, T], I32, name="x_word_table", align_bytes=64)
         nc.sync.dma_start(x_word_table[:], x_words[0].rearrange("p n t -> p (n t)").bitcast(I32))
+        nc.sync.dma_start(d_byte_table[0:P:8, :].bitcast(I32), d_scales[0].bitcast(I32))
+        nc.sync.dma_start(x_byte_table[0:P:8, :].bitcast(I32), x_scales[0].bitcast(I32))
         d_word_table = keep.tile([P, G], I32, name="d_word_table", align_bytes=64)
         nc.sync.dma_start(d_word_table[:], d_words[0].rearrange("p n t -> p (n t)").bitcast(I32))
         cand_list = load_list(cand, "cand_list")
         gain = keep.tile([P, PACK], F32, name="gain")
-        nc.gpsimd.dma_start(gain[:], gs.rearrange("(p t) o -> p (t o)", t=PACK))
+        nc.scalar.dma_start(gain[:], gs.rearrange("(p t) o -> p (t o)", t=PACK))
         n1_list = load_list(n1, "n1_list")
         n2_list = load_list(n2, "n2_list")
         n4_list = load_list(n4, "n4_list")
@@ -77,42 +77,55 @@ def tile_picked_pqcminmxpagez_none_po_kernel(
         zero_bytes(cand_placed)
         rows = [keep.tile([P, 2 * S], F32, name="rows%d" % t) for t in range(PACK)]
         nc.vector.memset(rows[0][:, S:], 0.0)
-        pages = [keep.tile([P, U], F32, name="page%d" % i) for i in range(2)]
-        for page in pages:
-            nc.vector.memset(page[:], 0.0)
+        first_page = keep.tile([P, U], F32, name="page0")
+        nc.vector.memset(first_page[:], 0.0)
 
-        first_picked = keep.tile([P, H + S], U8, name="first_picked", align_bytes=64)
-        nc.vector.tensor_copy(first_picked[:, H:], x_byte_table[:].indirect(offs_list[:]))
+        first_picked = keep.tile([P, H + S], U8, name="first_picked", tag="picked_bytes", align_bytes=64)
         nc.vector.tensor_copy(first_picked[:, :H], d_byte_table[:].indirect(k1_list[:]))
+        nc.vector.tensor_copy(first_picked[:, H:], x_byte_table[:].indirect(offs_list[:]))
         place_scale_rows(first_placed, first_picked)
-        d_picked = keep.tile([P, H], U32, name="d_picked", tag="d_bytes_then_words", align_bytes=64)
-        nc.vector.tensor_copy(d_picked[:], d_word_table[:].bitcast(U32).indirect(k1_list[:]))
-        token_words = keep.tile([P, S], U32, name="token_words", align_bytes=64)
+        token_words = keep.tile([P, S], U32, name="token_words", tag="d_bytes_then_words", align_bytes=64)
         nc.vector.tensor_copy(token_words[:], x_word_table[:].bitcast(U32).indirect(offs_list[:]))
+        d_picked = keep.tile([P, H], U32, name="d_picked", align_bytes=64)
+        nc.vector.tensor_copy(d_picked[:], d_word_table[:].bitcast(U32).indirect(k1_list[:]))
         d_dealt = keep.tile([P, H], U32, name="d_dealt", align_bytes=64)
         deal(d_dealt[:], d_picked[:])
         d_scale_dealt = keep.tile([P, H], U8, name="d_scale_dealt", align_bytes=64)
         deal(d_scale_dealt[:], first_placed[:, :H])
 
-        cand_bytes = keep.tile([P, C], U8, name="cand_bytes", align_bytes=64)
+        cand_bytes = keep.tile([P, C], U8, name="cand_bytes", tag="picked_bytes", align_bytes=64)
         nc.vector.tensor_copy(cand_bytes[:], x_byte_table[:].indirect(cand_list[:]))
         place_scale_rows(cand_placed, cand_bytes)
 
-        for t in range(PACK):
-            cols = slice(t * P, (t + 1) * P)
-            h_bank = psum.tile([P, S], F32, name="h_bank%d" % t)
-            nc.tensor.matmul_mx(
-                out=h_bank[:],
-                lhsT=d_dealt[:, cols].bitcast(FP8X4),
-                lhsT_scale=d_scale_dealt[:, cols],
-                rhs=token_words[:].bitcast(FP8X4),
-                rhs_scale=first_placed[:, H:],
-                start=True,
-                stop=True,
-            )
-            nc.scalar.activation(rows[t][:, :S], h_bank[:], ACT.Copy, scale=SIXTEENTH)
+        def product(t, stationary, stationary_scales, moving, moving_scales):
+            rows_t = slice(t * P, (t + 1) * P)
+            pieces = [slice(0, HALF), slice(HALF, S)] if t == 0 else [slice(0, S)]
+            banks = []
+            for i, cols in enumerate(pieces):
+                bank = psum.tile([P, cols.stop - cols.start], F32, name="bank", tag="bank%d_%d" % (t, i))
+                nc.tensor.matmul_mx(
+                    out=bank[:],
+                    lhsT=stationary[:, rows_t].bitcast(FP8X4),
+                    lhsT_scale=stationary_scales[:, rows_t],
+                    rhs=moving[:, cols].bitcast(FP8X4),
+                    rhs_scale=moving_scales[:, cols],
+                    start=True,
+                    stop=True,
+                )
+                banks.append((cols, bank))
+            return banks
 
-        z_grouped = keep.tile([P, S, PACK], BF16, name="z_grouped", tag="z_then_page", align_bytes=64)
+        def empty(target, banks, func):
+            for cols, bank in banks:
+                nc.scalar.activation(target[:, cols], bank[:], func, scale=SIXTEENTH)
+
+        for t in range(PACK):
+            empty(rows[t], product(t, d_dealt, d_scale_dealt, token_words, first_placed[:, H:]), ACT.Copy)
+
+        z_grouped = [
+            keep.tile([P, HALF, PACK], BF16, name="z_grouped%d" % i, tag="z_then_page%d" % i, align_bytes=64)
+            for i in range(2)
+        ]
         last_first = keep.tile([P, S], F32, name="last_first", tag="last_then_cand", align_bytes=64)
         firsts = [rows[t + 1][:, S:] for t in range(PACK - 1)] + [last_first[:]]
         seconds = [keep.tile([P, S], F32, name="second%d" % t) for t in range(PACK)]
@@ -121,7 +134,10 @@ def tile_picked_pqcminmxpagez_none_po_kernel(
 
         def finish_z(t):
             nc.vector.tensor_tensor(smaller[t][:], larger[t][:], seconds[t][:], ALU.min)
-            nc.scalar.activation(z_grouped[:, :, t], smaller[t][:], ACT.Copy, scale=gain[:, t : t + 1])
+            for i in range(2):
+                nc.scalar.activation(
+                    z_grouped[i][:, :, t], smaller[t][:, i * HALF : (i + 1) * HALF], ACT.Copy, scale=gain[:, t : t + 1]
+                )
 
         for t in range(PACK):
             nc.vector.tensor_copy(firsts[t], rows[t][:].indirect(n1_list[:]))
@@ -140,32 +156,27 @@ def tile_picked_pqcminmxpagez_none_po_kernel(
 
         z_words = keep.tile([P, S], U32, name="z_words", align_bytes=64)
         z_scales = keep.tile([P, S], U8, name="z_scales", align_bytes=64)
-        nc.vector.quantize_mx(
-            out=z_words[:].bitcast(FP8X4), scales=z_scales[:], in_=z_grouped[:].rearrange("p s t -> p (s t)")
-        )
-        third_page = keep.tile([P, U], F32, name="page2", tag="z_then_page", align_bytes=64)
-        nc.vector.memset(third_page[:], 0.0)
-        pages.append(third_page)
-
-        s_banks = []
-        scores = [keep.tile([P, S], F32, name="score%d" % t) for t in range(PACK)]
-        for t in range(PACK):
-            cols = slice(t * P, (t + 1) * P)
-            s_bank = psum.tile([P, S], F32, name="s_bank%d" % t)
-            nc.tensor.matmul_mx(
-                out=s_bank[:],
-                lhsT=cand_dealt[:, cols].bitcast(FP8X4),
-                lhsT_scale=cand_scale_dealt[:, cols],
-                rhs=z_words[:].bitcast(FP8X4),
-                rhs_scale=z_scales[:],
-                start=True,
-                stop=True,
+        for i in range(2):
+            cols = slice(i * HALF, (i + 1) * HALF)
+            nc.vector.quantize_mx(
+                out=z_words[:, cols].bitcast(FP8X4),
+                scales=z_scales[:, cols],
+                in_=z_grouped[i][:].rearrange("p s t -> p (s t)"),
             )
-            s_banks.append(s_bank)
-            nc.scalar.activation(rows[t][:, :S], s_bank[:], ACT.Relu, scale=SIXTEENTH)
+        pages = [first_page]
+        for i in range(2):
+            page = keep.tile([P, U], F32, name="page%d" % (i + 1), tag="z_then_page%d" % i, align_bytes=64)
+            nc.vector.memset(page[:], 0.0)
+            pages.append(page)
+
+        scores = [keep.tile([P, S], F32, name="score%d" % t) for t in range(PACK)]
+        s_banks = []
+        for t in range(PACK):
+            s_banks.append(product(t, cand_dealt, cand_scale_dealt, z_words, z_scales))
+            empty(rows[t], s_banks[t], ACT.Relu)
             if t > 0:
-                nc.scalar.activation(scores[t - 1][:], s_banks[t - 1][:], ACT.Copy, scale=SIXTEENTH)
-        nc.scalar.activation(scores[PACK - 1][:], s_banks[PACK - 1][:], ACT.Copy, scale=SIXTEENTH)
+                empty(scores[t - 1], s_banks[t - 1], ACT.Copy)
+        empty(scores[PACK - 1], s_banks[PACK - 1], ACT.Copy)
 
         grouped = [keep.tile([P, CHUNK, PACK], BF16, name="grouped%d" % c, align_bytes=64) for c in range(CHUNKS)]
         out_words = keep.tile([P, U], U32, name="out_words", align_bytes=64)
@@ -200,9 +211,9 @@ def tile_picked_pqcminmxpagez_none_po_kernel(
                 scales=out_scales[:, cols],
                 in_=grouped[c][:].rearrange("p u t -> p (u t)"),
             )
-            if c % 2 == 1:
-                pair = slice((c - 1) * CHUNK, (c + 1) * CHUNK)
-                nc.sync.dma_start(out_word_rows[:, pair], out_words[:, pair].bitcast(I32))
+            if c > 0:
+                done = slice(0 if c == 1 else c * CHUNK, (c + 1) * CHUNK)
+                nc.sync.dma_start(out_word_rows[:, done], out_words[:, done].bitcast(I32))
         for q in range(PACK):
             queue = nc.scalar if q % 2 == 0 else nc.sync
             queue.dma_start(out_2[0, 4 * q : 4 * q + 4, :].bitcast(I32), out_scales[32 * q : 32 * q + 4, :].bitcast(I32))

@@ -18,10 +18,12 @@ ACT = mybir.ActivationFunctionType
 P = 128
 PACK = 4
 SIXTEENTH = 0.0625
-HALF = S // 2
-CHUNK = 256
-CHUNKS = U // CHUNK
-VECTOR_CHUNKS = 2
+WHOLE = [slice(0, S)]
+H_PIECES = [slice(0, S // 2), slice(S // 2, S)]
+Z_PIECES = [slice(0, S // 2), slice(S // 2, 3 * S // 4), slice(3 * S // 4, S)]
+PAGES = 3
+VECTOR_PIECE = slice(0, U // 2)
+PAGE_PIECES = [slice(U // 2, 3 * U // 4), VECTOR_PIECE, slice(3 * U // 4, U)]
 
 
 def tile_picked_pqcminmxpagez_none_po_kernel(
@@ -39,74 +41,79 @@ def tile_picked_pqcminmxpagez_none_po_kernel(
             return tile
 
         def zero_bytes(tile):
-            nc.vector.memset(tile[:].bitcast(I32), 0)
+            nc.gpsimd.memset(tile.bitcast(I32), 0)
 
-        def place_scale_rows(placed, picked):
+        def place_scale_rows(placed, picked, queues):
             for c in range(PACK):
-                nc.sync.dma_start(placed[c:P:32, :].bitcast(I32), picked[8 * c : P : 32, :].bitcast(I32))
+                queues[c % len(queues)].dma_start(placed[c:P:32, :].bitcast(I32), picked[8 * c : P : 32, :].bitcast(I32))
 
-        def deal(dealt, picked):
+        def deal_pair(dealt, picked, first):
             nc.vector.tensor_copy(
-                out=dealt.rearrange("p (t m) -> p m t", t=PACK), in_=picked.rearrange("p (m t) -> p m t", t=PACK)
+                out=dealt.rearrange("p (t m) -> p m t", t=2),
+                in_=picked.rearrange("p (m t) -> p m t", t=PACK)[:, :, first : first + 2],
             )
 
         x_byte_table = keep.tile([P, T], U8, name="x_byte_table", align_bytes=64)
         d_byte_table = keep.tile([P, G], U8, name="d_byte_table", tag="d_bytes_then_words", align_bytes=64)
-        zero_bytes(d_byte_table)
-        zero_bytes(x_byte_table)
+        nc.vector.memset(d_byte_table[:, : G // 2].bitcast(I32), 0)
+        zero_bytes(d_byte_table[:, G // 2 :])
+        nc.vector.memset(x_byte_table[:].bitcast(I32), 0)
 
         k1_list = load_list(k1, "k1_list")
         offs_list = load_list(offs, "offs_list")
-        x_word_table = keep.tile([P, T], I32, name="x_word_table", align_bytes=64)
-        nc.sync.dma_start(x_word_table[:], x_words[0].rearrange("p n t -> p (n t)").bitcast(I32))
         nc.sync.dma_start(d_byte_table[0:P:8, :].bitcast(I32), d_scales[0].bitcast(I32))
         nc.sync.dma_start(x_byte_table[0:P:8, :].bitcast(I32), x_scales[0].bitcast(I32))
+        cand_list = load_list(cand, "cand_list")
+        n1_list = load_list(n1, "n1_list")
+        x_word_table = keep.tile([P, T], I32, name="x_word_table", align_bytes=64)
+        nc.sync.dma_start(x_word_table[:], x_words[0].rearrange("p n t -> p (n t)").bitcast(I32))
         d_word_table = keep.tile([P, G], I32, name="d_word_table", align_bytes=64)
         nc.sync.dma_start(d_word_table[:], d_words[0].rearrange("p n t -> p (n t)").bitcast(I32))
-        cand_list = load_list(cand, "cand_list")
-        gain = keep.tile([P, PACK], F32, name="gain")
-        nc.scalar.dma_start(gain[:], gs.rearrange("(p t) o -> p (t o)", t=PACK))
-        n1_list = load_list(n1, "n1_list")
         n2_list = load_list(n2, "n2_list")
+        gain = keep.tile([P, PACK], F32, name="gain")
+        nc.sync.dma_start(gain[:], gs.rearrange("(p t) o -> p (t o)", t=PACK))
         n4_list = load_list(n4, "n4_list")
         n3_list = load_list(n3, "n3_list")
 
         first_placed = keep.tile([P, H + S], U8, name="first_placed", align_bytes=64)
         cand_placed = keep.tile([P, C], U8, name="cand_placed", align_bytes=64)
-        zero_bytes(first_placed)
-        zero_bytes(cand_placed)
+        zero_bytes(first_placed[:])
         rows = [keep.tile([P, 2 * S], F32, name="rows%d" % t) for t in range(PACK)]
-        nc.vector.memset(rows[0][:, S:], 0.0)
-        first_page = keep.tile([P, U], F32, name="page0")
-        nc.vector.memset(first_page[:], 0.0)
+        nc.gpsimd.memset(rows[0][:, S:], 0.0)
+        zero_bytes(cand_placed[:])
+        pages = [keep.tile([P, U], F32, name="page%d" % i) for i in range(PAGES)]
+        for page in pages:
+            nc.gpsimd.memset(page[:], 0.0)
 
         first_picked = keep.tile([P, H + S], U8, name="first_picked", tag="picked_bytes", align_bytes=64)
         nc.vector.tensor_copy(first_picked[:, :H], d_byte_table[:].indirect(k1_list[:]))
         nc.vector.tensor_copy(first_picked[:, H:], x_byte_table[:].indirect(offs_list[:]))
-        place_scale_rows(first_placed, first_picked)
+        place_scale_rows(first_placed, first_picked, [nc.sync, nc.scalar])
         token_words = keep.tile([P, S], U32, name="token_words", tag="d_bytes_then_words", align_bytes=64)
         nc.vector.tensor_copy(token_words[:], x_word_table[:].bitcast(U32).indirect(offs_list[:]))
-        d_picked = keep.tile([P, H], U32, name="d_picked", align_bytes=64)
+        d_picked = keep.tile([P, H], U32, name="d_picked", tag="d_picked", align_bytes=64)
         nc.vector.tensor_copy(d_picked[:], d_word_table[:].bitcast(U32).indirect(k1_list[:]))
-        d_dealt = keep.tile([P, H], U32, name="d_dealt", align_bytes=64)
-        deal(d_dealt[:], d_picked[:])
+        d_early = keep.tile([P, H // 2], U32, name="d_early", align_bytes=64)
+        deal_pair(d_early[:], d_picked[:], 0)
         d_scale_dealt = keep.tile([P, H], U8, name="d_scale_dealt", align_bytes=64)
-        deal(d_scale_dealt[:], first_placed[:, :H])
+        deal_pair(d_scale_dealt[:, : H // 2], first_placed[:, :H], 0)
+        d_late = keep.tile([P, H // 2], U32, name="d_late", tag="picked_bytes", align_bytes=64)
+        deal_pair(d_late[:], d_picked[:], 2)
+        deal_pair(d_scale_dealt[:, H // 2 :], first_placed[:, :H], 2)
+        d_tiles = [pair[:, i * P : (i + 1) * P] for pair in (d_early, d_late) for i in range(2)]
 
-        cand_bytes = keep.tile([P, C], U8, name="cand_bytes", tag="picked_bytes", align_bytes=64)
+        cand_bytes = keep.tile([P, C], U8, name="cand_bytes", tag="d_picked", align_bytes=64)
         nc.vector.tensor_copy(cand_bytes[:], x_byte_table[:].indirect(cand_list[:]))
-        place_scale_rows(cand_placed, cand_bytes)
+        place_scale_rows(cand_placed, cand_bytes, [nc.sync])
 
-        def product(t, stationary, stationary_scales, moving, moving_scales):
-            rows_t = slice(t * P, (t + 1) * P)
-            pieces = [slice(0, HALF), slice(HALF, S)] if t == 0 else [slice(0, S)]
+        def product(t, pieces, stationary, stationary_scales, moving, moving_scales):
             banks = []
             for i, cols in enumerate(pieces):
                 bank = psum.tile([P, cols.stop - cols.start], F32, name="bank", tag="bank%d_%d" % (t, i))
                 nc.tensor.matmul_mx(
                     out=bank[:],
-                    lhsT=stationary[:, rows_t].bitcast(FP8X4),
-                    lhsT_scale=stationary_scales[:, rows_t],
+                    lhsT=stationary.bitcast(FP8X4),
+                    lhsT_scale=stationary_scales,
                     rhs=moving[:, cols].bitcast(FP8X4),
                     rhs_scale=moving_scales[:, cols],
                     start=True,
@@ -120,24 +127,27 @@ def tile_picked_pqcminmxpagez_none_po_kernel(
                 nc.scalar.activation(target[:, cols], bank[:], func, scale=SIXTEENTH)
 
         for t in range(PACK):
-            empty(rows[t], product(t, d_dealt, d_scale_dealt, token_words, first_placed[:, H:]), ACT.Copy)
+            cols = slice(t * P, (t + 1) * P)
+            pieces = H_PIECES if t == 0 else WHOLE
+            banks = product(t, pieces, d_tiles[t], d_scale_dealt[:, cols], token_words, first_placed[:, H:])
+            empty(rows[t], banks, ACT.Copy)
 
         z_grouped = [
-            keep.tile([P, HALF, PACK], BF16, name="z_grouped%d" % i, tag="z_then_page%d" % i, align_bytes=64)
-            for i in range(2)
+            keep.tile([P, cols.stop - cols.start, PACK], BF16, name="z_grouped", tag="z_grouped%d" % i, align_bytes=64)
+            for i, cols in enumerate(Z_PIECES)
         ]
         last_first = keep.tile([P, S], F32, name="last_first", tag="last_then_cand", align_bytes=64)
         firsts = [rows[t + 1][:, S:] for t in range(PACK - 1)] + [last_first[:]]
         seconds = [keep.tile([P, S], F32, name="second%d" % t) for t in range(PACK)]
-        larger = [keep.tile([P, S], F32, name="larger%d" % t) for t in range(PACK)]
-        smaller = [keep.tile([P, S], F32, name="smaller%d" % t) for t in range(PACK)]
+        larger = [keep.tile([P, S], F32, name="larger%d" % t, tag="larger%d" % t, align_bytes=64) for t in range(PACK)]
+        smaller = [keep.tile([P, S], F32, name="smaller%d" % t, tag="smaller%d" % t, align_bytes=64) for t in range(PACK)]
 
         def finish_z(t):
-            nc.vector.tensor_tensor(smaller[t][:], larger[t][:], seconds[t][:], ALU.min)
-            for i in range(2):
-                nc.scalar.activation(
-                    z_grouped[i][:, :, t], smaller[t][:, i * HALF : (i + 1) * HALF], ACT.Copy, scale=gain[:, t : t + 1]
-                )
+            pieces = H_PIECES if t == PACK - 1 else WHOLE
+            for cols in pieces:
+                nc.vector.tensor_tensor(smaller[t][:, cols], larger[t][:, cols], seconds[t][:, cols], ALU.min)
+            for i, cols in enumerate(Z_PIECES):
+                nc.scalar.activation(z_grouped[i][:, :, t], smaller[t][:, cols], ACT.Copy, scale=gain[:, t : t + 1])
 
         for t in range(PACK):
             nc.vector.tensor_copy(firsts[t], rows[t][:].indirect(n1_list[:]))
@@ -149,36 +159,40 @@ def tile_picked_pqcminmxpagez_none_po_kernel(
 
         cand_picked = keep.tile([P, C], U32, name="cand_picked", tag="last_then_cand", align_bytes=64)
         nc.vector.tensor_copy(cand_picked[:], x_word_table[:].bitcast(U32).indirect(cand_list[:]))
-        cand_scale_dealt = keep.tile([P, C], U8, name="cand_scale_dealt", align_bytes=64)
-        deal(cand_scale_dealt[:], cand_placed[:])
-        cand_dealt = keep.tile([P, C], U32, name="cand_dealt", align_bytes=64)
-        deal(cand_dealt[:], cand_picked[:])
+        cand_scale_0 = keep.tile([P, C // 2], U8, name="cand_scale_0", tag="larger3", align_bytes=64)
+        deal_pair(cand_scale_0[:], cand_placed[:], 0)
+        cand_0 = keep.tile([P, C // 2], U32, name="cand_0", align_bytes=64)
+        deal_pair(cand_0[:], cand_picked[:], 0)
 
         z_words = keep.tile([P, S], U32, name="z_words", align_bytes=64)
         z_scales = keep.tile([P, S], U8, name="z_scales", align_bytes=64)
-        for i in range(2):
-            cols = slice(i * HALF, (i + 1) * HALF)
+        for i, cols in enumerate(Z_PIECES):
             nc.vector.quantize_mx(
                 out=z_words[:, cols].bitcast(FP8X4),
                 scales=z_scales[:, cols],
                 in_=z_grouped[i][:].rearrange("p s t -> p (s t)"),
             )
-        pages = [first_page]
-        for i in range(2):
-            page = keep.tile([P, U], F32, name="page%d" % (i + 1), tag="z_then_page%d" % i, align_bytes=64)
-            nc.vector.memset(page[:], 0.0)
-            pages.append(page)
+
+        cand_scale_rest = keep.tile([P, C // 2], U8, name="cand_scale_rest", tag="smaller3", align_bytes=64)
+        deal_pair(cand_scale_rest[:], cand_placed[:], 2)
+        cand_rest = keep.tile([P, C // 2], U32, name="cand_rest", tag="z_grouped2", align_bytes=64)
+        deal_pair(cand_rest[:], cand_picked[:], 2)
+        cand_tiles = [pair[:, i * P : (i + 1) * P] for pair in (cand_0, cand_rest) for i in range(2)]
+        cand_scale_tiles = [pair[:, i * P : (i + 1) * P] for pair in (cand_scale_0, cand_scale_rest) for i in range(2)]
 
         scores = [keep.tile([P, S], F32, name="score%d" % t) for t in range(PACK)]
         s_banks = []
         for t in range(PACK):
-            s_banks.append(product(t, cand_dealt, cand_scale_dealt, z_words, z_scales))
+            s_banks.append(product(t, Z_PIECES if t == 0 else WHOLE, cand_tiles[t], cand_scale_tiles[t], z_words, z_scales))
             empty(rows[t], s_banks[t], ACT.Relu)
             if t > 0:
                 empty(scores[t - 1], s_banks[t - 1], ACT.Copy)
         empty(scores[PACK - 1], s_banks[PACK - 1], ACT.Copy)
 
-        grouped = [keep.tile([P, CHUNK, PACK], BF16, name="grouped%d" % c, align_bytes=64) for c in range(CHUNKS)]
+        grouped = [
+            keep.tile([P, cols.stop - cols.start, PACK], BF16, name="grouped%d" % i, align_bytes=64)
+            for i, cols in enumerate(PAGE_PIECES)
+        ]
         out_words = keep.tile([P, U], U32, name="out_words", align_bytes=64)
         out_scales = keep.tile([P, U], U8, name="out_scales", align_bytes=64)
         out_rows = out_0.rearrange("(p t) u -> t p u", t=PACK)
@@ -194,26 +208,23 @@ def tile_picked_pqcminmxpagez_none_po_kernel(
             page = pages[t % len(pages)]
             nc.vector.tensor_tensor(page[:].indirect(n3_list[:]), scores[t][:], negated[t][:], ALU.add)
             nc.sync.dma_start(out_rows[t], page[:])
-            for c in range(CHUNKS):
-                piece = page[:, c * CHUNK : (c + 1) * CHUNK]
-                if c < VECTOR_CHUNKS and t == PACK - 2:
-                    nc.scalar.copy(grouped[c][:, :, t:], piece.unsqueeze(2).broadcast_to([P, CHUNK, 2]))
-                elif c < VECTOR_CHUNKS and t == PACK - 1:
-                    nc.vector.tensor_copy(grouped[c][:, :, t], piece)
+            for i, cols in enumerate(PAGE_PIECES):
+                if cols == VECTOR_PIECE and t == PACK - 2:
+                    twice = page[:, cols].unsqueeze(2).broadcast_to([P, cols.stop - cols.start, 2])
+                    nc.scalar.copy(grouped[i][:, :, t:], twice)
+                elif cols == VECTOR_PIECE and t == PACK - 1:
+                    nc.vector.tensor_copy(grouped[i][:, :, t], page[:, cols])
                 else:
-                    nc.scalar.copy(grouped[c][:, :, t], piece)
+                    nc.scalar.copy(grouped[i][:, :, t], page[:, cols])
 
         out_word_rows = out_1[0].rearrange("p u t -> p (u t)").bitcast(I32)
-        for c in range(CHUNKS):
-            cols = slice(c * CHUNK, (c + 1) * CHUNK)
+        for i, cols in enumerate(PAGE_PIECES):
             nc.vector.quantize_mx(
                 out=out_words[:, cols].bitcast(FP8X4),
                 scales=out_scales[:, cols],
-                in_=grouped[c][:].rearrange("p u t -> p (u t)"),
+                in_=grouped[i][:].rearrange("p u t -> p (u t)"),
             )
-            if c > 0:
-                done = slice(0 if c == 1 else c * CHUNK, (c + 1) * CHUNK)
-                nc.sync.dma_start(out_word_rows[:, done], out_words[:, done].bitcast(I32))
+            nc.sync.dma_start(out_word_rows[:, cols], out_words[:, cols].bitcast(I32))
         for q in range(PACK):
             queue = nc.scalar if q % 2 == 0 else nc.sync
             queue.dma_start(out_2[0, 4 * q : 4 * q + 4, :].bitcast(I32), out_scales[32 * q : 32 * q + 4, :].bitcast(I32))

@@ -17,13 +17,21 @@ ACT = mybir.ActivationFunctionType
 
 P = 128
 PACK = 4
+LAST = PACK - 1
+GROUP = 16
+BLOCK_PARTITIONS = 8
+QUADRANT = 32
 SIXTEENTH = 0.0625
+
 WHOLE = [slice(0, S)]
-H_PIECES = [slice(0, S // 2), slice(S // 2, S)]
+HALVES = [slice(0, S // 2), slice(S // 2, S)]
 Z_PIECES = [slice(0, S // 2), slice(S // 2, 3 * S // 4), slice(3 * S // 4, S)]
-PAGES = 3
 VECTOR_PIECE = slice(0, U // 2)
 PAGE_PIECES = [slice(U // 2, 3 * U // 4), VECTOR_PIECE, slice(3 * U // 4, U)]
+
+
+def width(cols):
+    return cols.stop - cols.start
 
 
 def tile_picked_pqcminmxpagez_none_po_kernel(
@@ -36,16 +44,18 @@ def tile_picked_pqcminmxpagez_none_po_kernel(
         psum = ctx.enter_context(tc.psum_pool(name="psum", bufs=1))
 
         def load_list(source, name):
-            tile = lists.tile([P, S // 16], U16, name=name)
+            tile = lists.tile([P, S // GROUP], U16, name=name)
             nc.sync.dma_start(tile[:], source)
             return tile
 
         def zero_bytes(tile):
-            nc.gpsimd.memset(tile.bitcast(I32), 0)
+            nc.vector.memset(tile[:].bitcast(I32), 0)
 
-        def place_scale_rows(placed, picked, queues):
+        def place_scale_rows(placed, picked):
             for c in range(PACK):
-                queues[c % len(queues)].dma_start(placed[c:P:32, :].bitcast(I32), picked[8 * c : P : 32, :].bitcast(I32))
+                nc.sync.dma_start(
+                    placed[c:P:QUADRANT, :].bitcast(I32), picked[BLOCK_PARTITIONS * c : P : QUADRANT, :].bitcast(I32)
+                )
 
         def deal_pair(dealt, picked, first):
             nc.vector.tensor_copy(
@@ -53,63 +63,13 @@ def tile_picked_pqcminmxpagez_none_po_kernel(
                 in_=picked.rearrange("p (m t) -> p m t", t=PACK)[:, :, first : first + 2],
             )
 
-        x_byte_table = keep.tile([P, T], U8, name="x_byte_table", align_bytes=64)
-        d_byte_table = keep.tile([P, G], U8, name="d_byte_table", tag="d_bytes_then_words", align_bytes=64)
-        nc.vector.memset(d_byte_table[:, : G // 2].bitcast(I32), 0)
-        zero_bytes(d_byte_table[:, G // 2 :])
-        nc.vector.memset(x_byte_table[:].bitcast(I32), 0)
-
-        k1_list = load_list(k1, "k1_list")
-        offs_list = load_list(offs, "offs_list")
-        nc.sync.dma_start(d_byte_table[0:P:8, :].bitcast(I32), d_scales[0].bitcast(I32))
-        nc.sync.dma_start(x_byte_table[0:P:8, :].bitcast(I32), x_scales[0].bitcast(I32))
-        cand_list = load_list(cand, "cand_list")
-        n1_list = load_list(n1, "n1_list")
-        x_word_table = keep.tile([P, T], I32, name="x_word_table", align_bytes=64)
-        nc.sync.dma_start(x_word_table[:], x_words[0].rearrange("p n t -> p (n t)").bitcast(I32))
-        d_word_table = keep.tile([P, G], I32, name="d_word_table", align_bytes=64)
-        nc.sync.dma_start(d_word_table[:], d_words[0].rearrange("p n t -> p (n t)").bitcast(I32))
-        n2_list = load_list(n2, "n2_list")
-        gain = keep.tile([P, PACK], F32, name="gain")
-        nc.sync.dma_start(gain[:], gs.rearrange("(p t) o -> p (t o)", t=PACK))
-        n4_list = load_list(n4, "n4_list")
-        n3_list = load_list(n3, "n3_list")
-
-        first_placed = keep.tile([P, H + S], U8, name="first_placed", align_bytes=64)
-        cand_placed = keep.tile([P, C], U8, name="cand_placed", align_bytes=64)
-        zero_bytes(first_placed[:])
-        rows = [keep.tile([P, 2 * S], F32, name="rows%d" % t) for t in range(PACK)]
-        nc.gpsimd.memset(rows[0][:, S:], 0.0)
-        zero_bytes(cand_placed[:])
-        pages = [keep.tile([P, U], F32, name="page%d" % i) for i in range(PAGES)]
-        for page in pages:
-            nc.gpsimd.memset(page[:], 0.0)
-
-        first_picked = keep.tile([P, H + S], U8, name="first_picked", tag="picked_bytes", align_bytes=64)
-        nc.vector.tensor_copy(first_picked[:, :H], d_byte_table[:].indirect(k1_list[:]))
-        nc.vector.tensor_copy(first_picked[:, H:], x_byte_table[:].indirect(offs_list[:]))
-        place_scale_rows(first_placed, first_picked, [nc.sync, nc.scalar])
-        token_words = keep.tile([P, S], U32, name="token_words", tag="d_bytes_then_words", align_bytes=64)
-        nc.vector.tensor_copy(token_words[:], x_word_table[:].bitcast(U32).indirect(offs_list[:]))
-        d_picked = keep.tile([P, H], U32, name="d_picked", tag="d_picked", align_bytes=64)
-        nc.vector.tensor_copy(d_picked[:], d_word_table[:].bitcast(U32).indirect(k1_list[:]))
-        d_early = keep.tile([P, H // 2], U32, name="d_early", align_bytes=64)
-        deal_pair(d_early[:], d_picked[:], 0)
-        d_scale_dealt = keep.tile([P, H], U8, name="d_scale_dealt", align_bytes=64)
-        deal_pair(d_scale_dealt[:, : H // 2], first_placed[:, :H], 0)
-        d_late = keep.tile([P, H // 2], U32, name="d_late", tag="picked_bytes", align_bytes=64)
-        deal_pair(d_late[:], d_picked[:], 2)
-        deal_pair(d_scale_dealt[:, H // 2 :], first_placed[:, :H], 2)
-        d_tiles = [pair[:, i * P : (i + 1) * P] for pair in (d_early, d_late) for i in range(2)]
-
-        cand_bytes = keep.tile([P, C], U8, name="cand_bytes", tag="d_picked", align_bytes=64)
-        nc.vector.tensor_copy(cand_bytes[:], x_byte_table[:].indirect(cand_list[:]))
-        place_scale_rows(cand_placed, cand_bytes, [nc.sync])
+        def by_row_tile(early_pair, late_pair):
+            return [pair[:, i * P : (i + 1) * P] for pair in (early_pair, late_pair) for i in range(2)]
 
         def product(t, pieces, stationary, stationary_scales, moving, moving_scales):
             banks = []
             for i, cols in enumerate(pieces):
-                bank = psum.tile([P, cols.stop - cols.start], F32, name="bank", tag="bank%d_%d" % (t, i))
+                bank = psum.tile([P, width(cols)], F32, name="bank", tag="bank%d_%d" % (t, i))
                 nc.tensor.matmul_mx(
                     out=bank[:],
                     lhsT=stationary.bitcast(FP8X4),
@@ -126,43 +86,92 @@ def tile_picked_pqcminmxpagez_none_po_kernel(
             for cols, bank in banks:
                 nc.scalar.activation(target[:, cols], bank[:], func, scale=SIXTEENTH)
 
+        x_byte_table = keep.tile([P, T], U8, name="x_byte_table", align_bytes=64)
+        d_byte_table = keep.tile([P, G], U8, name="d_byte_table", tag="d_bytes_then_tokens", align_bytes=64)
+        zero_bytes(d_byte_table)
+        zero_bytes(x_byte_table)
+
+        k1_list = load_list(k1, "k1_list")
+        offs_list = load_list(offs, "offs_list")
+        nc.sync.dma_start(d_byte_table[0:P:BLOCK_PARTITIONS, :].bitcast(I32), d_scales[0].bitcast(I32))
+        nc.sync.dma_start(x_byte_table[0:P:BLOCK_PARTITIONS, :].bitcast(I32), x_scales[0].bitcast(I32))
+        cand_list = load_list(cand, "cand_list")
+        n1_list = load_list(n1, "n1_list")
+        x_word_table = keep.tile([P, T], I32, name="x_word_table", align_bytes=64)
+        nc.sync.dma_start(x_word_table[:], x_words[0].rearrange("p n t -> p (n t)").bitcast(I32))
+        d_word_table = keep.tile([P, G], I32, name="d_word_table", align_bytes=64)
+        nc.sync.dma_start(d_word_table[:], d_words[0].rearrange("p n t -> p (n t)").bitcast(I32))
+        n2_list = load_list(n2, "n2_list")
+        gain = keep.tile([P, PACK], F32, name="gain")
+        nc.sync.dma_start(gain[:], gs.rearrange("(p t) o -> p (t o)", t=PACK))
+        n4_list = load_list(n4, "n4_list")
+        n3_list = load_list(n3, "n3_list")
+
+        first_placed = keep.tile([P, H + S], U8, name="first_placed", align_bytes=64)
+        cand_placed = keep.tile([P, C], U8, name="cand_placed", align_bytes=64)
+        zero_bytes(first_placed)
+        windows = [keep.tile([P, 2 * S], F32, name="window%d" % t) for t in range(PACK)]
+        nc.vector.memset(windows[0][:, S:], 0.0)
+        zero_bytes(cand_placed)
+        even_page = keep.tile([P, U], F32, name="even_page")
+        nc.vector.memset(even_page[:], 0.0)
+
+        first_picked = keep.tile([P, H + S], U8, name="first_picked", tag="bytes_then_d_late", align_bytes=64)
+        nc.vector.tensor_copy(first_picked[:, :H], d_byte_table[:].indirect(k1_list[:]))
+        nc.vector.tensor_copy(first_picked[:, H:], x_byte_table[:].indirect(offs_list[:]))
+        place_scale_rows(first_placed, first_picked)
+        token_words = keep.tile([P, S], U32, name="token_words", tag="d_bytes_then_tokens", align_bytes=64)
+        nc.vector.tensor_copy(token_words[:], x_word_table[:].bitcast(U32).indirect(offs_list[:]))
+        d_picked = keep.tile([P, H], U32, name="d_picked", tag="d_words_then_cand_bytes", align_bytes=64)
+        nc.vector.tensor_copy(d_picked[:], d_word_table[:].bitcast(U32).indirect(k1_list[:]))
+        d_early = keep.tile([P, H // 2], U32, name="d_early", align_bytes=64)
+        deal_pair(d_early[:], d_picked[:], 0)
+        d_scale_dealt = keep.tile([P, H], U8, name="d_scale_dealt", align_bytes=64)
+        deal_pair(d_scale_dealt[:, : H // 2], first_placed[:, :H], 0)
+        d_late = keep.tile([P, H // 2], U32, name="d_late", tag="bytes_then_d_late", align_bytes=64)
+        deal_pair(d_late[:], d_picked[:], 2)
+        deal_pair(d_scale_dealt[:, H // 2 :], first_placed[:, :H], 2)
+        d_tiles = by_row_tile(d_early, d_late)
+
+        cand_bytes = keep.tile([P, C], U8, name="cand_bytes", tag="d_words_then_cand_bytes", align_bytes=64)
+        nc.vector.tensor_copy(cand_bytes[:], x_byte_table[:].indirect(cand_list[:]))
+        place_scale_rows(cand_placed, cand_bytes)
+
         for t in range(PACK):
-            cols = slice(t * P, (t + 1) * P)
-            pieces = H_PIECES if t == 0 else WHOLE
-            banks = product(t, pieces, d_tiles[t], d_scale_dealt[:, cols], token_words, first_placed[:, H:])
-            empty(rows[t], banks, ACT.Copy)
+            d_scale_tile = d_scale_dealt[:, t * P : (t + 1) * P]
+            pieces = HALVES if t == 0 else WHOLE
+            empty(windows[t], product(t, pieces, d_tiles[t], d_scale_tile, token_words, first_placed[:, H:]), ACT.Copy)
 
         z_grouped = [
-            keep.tile([P, cols.stop - cols.start, PACK], BF16, name="z_grouped", tag="z_grouped%d" % i, align_bytes=64)
+            keep.tile([P, width(cols), PACK], BF16, name="z_grouped", tag="z_grouped%d" % i, align_bytes=64)
             for i, cols in enumerate(Z_PIECES)
         ]
-        last_first = keep.tile([P, S], F32, name="last_first", tag="last_then_cand", align_bytes=64)
-        firsts = [rows[t + 1][:, S:] for t in range(PACK - 1)] + [last_first[:]]
-        seconds = [keep.tile([P, S], F32, name="second%d" % t) for t in range(PACK)]
-        larger = [keep.tile([P, S], F32, name="larger%d" % t, tag="larger%d" % t, align_bytes=64) for t in range(PACK)]
-        smaller = [keep.tile([P, S], F32, name="smaller%d" % t, tag="smaller%d" % t, align_bytes=64) for t in range(PACK)]
+        last_at_n1 = keep.tile([P, S], F32, name="last_at_n1", tag="n1_then_cand_then_page", align_bytes=64)
+        at_n1 = [windows[t + 1][:, S:] for t in range(LAST)] + [last_at_n1[:]]
+        at_n2 = [keep.tile([P, S], F32, name="at_n2_%d" % t) for t in range(PACK)]
+        larger = [keep.tile([P, S], F32, name="larger", tag="larger%d" % t, align_bytes=64) for t in range(PACK)]
+        smaller = [keep.tile([P, S], F32, name="smaller", tag="smaller%d" % t, align_bytes=64) for t in range(PACK)]
 
         def finish_z(t):
-            pieces = H_PIECES if t == PACK - 1 else WHOLE
-            for cols in pieces:
-                nc.vector.tensor_tensor(smaller[t][:, cols], larger[t][:, cols], seconds[t][:, cols], ALU.min)
+            for cols in HALVES if t == LAST else WHOLE:
+                nc.vector.tensor_tensor(smaller[t][:, cols], larger[t][:, cols], at_n2[t][:, cols], ALU.min)
             for i, cols in enumerate(Z_PIECES):
                 nc.scalar.activation(z_grouped[i][:, :, t], smaller[t][:, cols], ACT.Copy, scale=gain[:, t : t + 1])
 
         for t in range(PACK):
-            nc.vector.tensor_copy(firsts[t], rows[t][:].indirect(n1_list[:]))
+            nc.vector.tensor_copy(at_n1[t], windows[t][:].indirect(n1_list[:]))
             if t > 0:
                 finish_z(t - 1)
-            nc.vector.tensor_copy(seconds[t][:], rows[t][:].indirect(n2_list[:]))
-            nc.vector.tensor_tensor(larger[t][:], rows[t][:, :S], firsts[t], ALU.max)
-        finish_z(PACK - 1)
+            nc.vector.tensor_copy(at_n2[t][:], windows[t][:].indirect(n2_list[:]))
+            nc.vector.tensor_tensor(larger[t][:], windows[t][:, :S], at_n1[t], ALU.max)
+        finish_z(LAST)
 
-        cand_picked = keep.tile([P, C], U32, name="cand_picked", tag="last_then_cand", align_bytes=64)
+        cand_picked = keep.tile([P, C], U32, name="cand_picked", tag="n1_then_cand_then_page", align_bytes=64)
         nc.vector.tensor_copy(cand_picked[:], x_word_table[:].bitcast(U32).indirect(cand_list[:]))
-        cand_scale_0 = keep.tile([P, C // 2], U8, name="cand_scale_0", tag="larger3", align_bytes=64)
-        deal_pair(cand_scale_0[:], cand_placed[:], 0)
-        cand_0 = keep.tile([P, C // 2], U32, name="cand_0", align_bytes=64)
-        deal_pair(cand_0[:], cand_picked[:], 0)
+        cand_scale_early = keep.tile([P, C // 2], U8, name="cand_scale_early", tag="larger%d" % LAST, align_bytes=64)
+        deal_pair(cand_scale_early[:], cand_placed[:], 0)
+        cand_early = keep.tile([P, C // 2], U32, name="cand_early", align_bytes=64)
+        deal_pair(cand_early[:], cand_picked[:], 0)
 
         z_words = keep.tile([P, S], U32, name="z_words", align_bytes=64)
         z_scales = keep.tile([P, S], U8, name="z_scales", align_bytes=64)
@@ -173,24 +182,30 @@ def tile_picked_pqcminmxpagez_none_po_kernel(
                 in_=z_grouped[i][:].rearrange("p s t -> p (s t)"),
             )
 
-        cand_scale_rest = keep.tile([P, C // 2], U8, name="cand_scale_rest", tag="smaller3", align_bytes=64)
-        deal_pair(cand_scale_rest[:], cand_placed[:], 2)
-        cand_rest = keep.tile([P, C // 2], U32, name="cand_rest", tag="z_grouped2", align_bytes=64)
-        deal_pair(cand_rest[:], cand_picked[:], 2)
-        cand_tiles = [pair[:, i * P : (i + 1) * P] for pair in (cand_0, cand_rest) for i in range(2)]
-        cand_scale_tiles = [pair[:, i * P : (i + 1) * P] for pair in (cand_scale_0, cand_scale_rest) for i in range(2)]
+        cand_scale_late = keep.tile([P, C // 2], U8, name="cand_scale_late", tag="smaller%d" % LAST, align_bytes=64)
+        deal_pair(cand_scale_late[:], cand_placed[:], 2)
+        last_z_tag = "z_grouped%d" % (len(Z_PIECES) - 1)
+        cand_late = keep.tile([P, C // 2], U32, name="cand_late", tag=last_z_tag, align_bytes=64)
+        deal_pair(cand_late[:], cand_picked[:], 2)
+        cand_tiles = by_row_tile(cand_early, cand_late)
+        cand_scale_tiles = by_row_tile(cand_scale_early, cand_scale_late)
+
+        odd_page = keep.tile([P, U], F32, name="odd_page", tag="n1_then_cand_then_page", align_bytes=64)
+        nc.vector.memset(odd_page[:], 0.0)
+        pages = [even_page, odd_page]
 
         scores = [keep.tile([P, S], F32, name="score%d" % t) for t in range(PACK)]
         s_banks = []
         for t in range(PACK):
-            s_banks.append(product(t, Z_PIECES if t == 0 else WHOLE, cand_tiles[t], cand_scale_tiles[t], z_words, z_scales))
-            empty(rows[t], s_banks[t], ACT.Relu)
+            pieces = Z_PIECES if t == 0 else WHOLE
+            s_banks.append(product(t, pieces, cand_tiles[t], cand_scale_tiles[t], z_words, z_scales))
+            empty(windows[t], s_banks[t], ACT.Relu)
             if t > 0:
                 empty(scores[t - 1], s_banks[t - 1], ACT.Copy)
-        empty(scores[PACK - 1], s_banks[PACK - 1], ACT.Copy)
+        empty(scores[LAST], s_banks[LAST], ACT.Copy)
 
-        grouped = [
-            keep.tile([P, cols.stop - cols.start, PACK], BF16, name="grouped%d" % i, align_bytes=64)
+        out_grouped = [
+            keep.tile([P, width(cols), PACK], BF16, name="out_grouped%d" % i, align_bytes=64)
             for i, cols in enumerate(PAGE_PIECES)
         ]
         out_words = keep.tile([P, U], U32, name="out_words", align_bytes=64)
@@ -199,32 +214,35 @@ def tile_picked_pqcminmxpagez_none_po_kernel(
         negated = [keep.tile([P, S], F32, name="negated%d" % t) for t in range(PACK)]
 
         def look_up(t):
-            nc.vector.tensor_scalar(negated[t][:], rows[t][:].indirect(n4_list[:]), -1.0, 0.0, ALU.mult, ALU.add)
+            nc.vector.tensor_scalar(negated[t][:], windows[t][:].indirect(n4_list[:]), -1.0, 0.0, ALU.mult, ALU.add)
 
         look_up(0)
         for t in range(PACK):
-            if t + 1 < PACK:
+            if t < LAST:
                 look_up(t + 1)
             page = pages[t % len(pages)]
             nc.vector.tensor_tensor(page[:].indirect(n3_list[:]), scores[t][:], negated[t][:], ALU.add)
             nc.sync.dma_start(out_rows[t], page[:])
             for i, cols in enumerate(PAGE_PIECES):
-                if cols == VECTOR_PIECE and t == PACK - 2:
-                    twice = page[:, cols].unsqueeze(2).broadcast_to([P, cols.stop - cols.start, 2])
-                    nc.scalar.copy(grouped[i][:, :, t:], twice)
-                elif cols == VECTOR_PIECE and t == PACK - 1:
-                    nc.vector.tensor_copy(grouped[i][:, :, t], page[:, cols])
+                if cols == VECTOR_PIECE and t == LAST - 1:
+                    twice = page[:, cols].unsqueeze(2).broadcast_to([P, width(cols), 2])
+                    nc.scalar.copy(out_grouped[i][:, :, t:], twice)
+                elif cols == VECTOR_PIECE and t == LAST:
+                    nc.vector.tensor_copy(out_grouped[i][:, :, t], page[:, cols])
                 else:
-                    nc.scalar.copy(grouped[i][:, :, t], page[:, cols])
+                    nc.scalar.copy(out_grouped[i][:, :, t], page[:, cols])
 
         out_word_rows = out_1[0].rearrange("p u t -> p (u t)").bitcast(I32)
         for i, cols in enumerate(PAGE_PIECES):
             nc.vector.quantize_mx(
                 out=out_words[:, cols].bitcast(FP8X4),
                 scales=out_scales[:, cols],
-                in_=grouped[i][:].rearrange("p u t -> p (u t)"),
+                in_=out_grouped[i][:].rearrange("p u t -> p (u t)"),
             )
             nc.sync.dma_start(out_word_rows[:, cols], out_words[:, cols].bitcast(I32))
-        for q in range(PACK):
+        for q in range(P // QUADRANT):
             queue = nc.scalar if q % 2 == 0 else nc.sync
-            queue.dma_start(out_2[0, 4 * q : 4 * q + 4, :].bitcast(I32), out_scales[32 * q : 32 * q + 4, :].bitcast(I32))
+            queue.dma_start(
+                out_2[0, PACK * q : PACK * (q + 1), :].bitcast(I32),
+                out_scales[QUADRANT * q : QUADRANT * q + PACK, :].bitcast(I32),
+            )

from contextlib import ExitStack

import concourse.mybir as mybir

K, T, S, G, H, C, U = 512, 1024, 512, 2048, 512, 512, 1024
FLOPS = 2 * K * H * S + 2 * K * C * S

F32 = mybir.dt.float32
BF16 = mybir.dt.bfloat16
I32 = mybir.dt.int32
U32 = mybir.dt.uint32
U16 = mybir.dt.uint16
U8 = mybir.dt.uint8
FP8X4 = mybir.dt.float8_e4m3fn_x4
ALU = mybir.AluOpType
ACT = mybir.ActivationFunctionType

P = 128
PACK = 4
LAST = PACK - 1
GROUP = 16
BLOCK_PARTITIONS = 8
QUADRANT = 32
SIXTEENTH = 0.0625

WHOLE = [slice(0, S)]
HALVES = [slice(0, S // 2), slice(S // 2, S)]
Z_PIECES = [slice(0, S // 2), slice(S // 2, 3 * S // 4), slice(3 * S // 4, S)]
VECTOR_PIECE = slice(0, U // 2)
PAGE_PIECES = [slice(U // 2, 3 * U // 4), VECTOR_PIECE, slice(3 * U // 4, U)]


def width(cols):
    return cols.stop - cols.start


def tile_picked_pqcminmxpagez_none_po_kernel(
    tc, x_words, x_scales, d_words, d_scales, gs, offs, k1, n1, n2, cand, n3, n4, out_0, out_1, out_2
):
    nc = tc.nc
    with ExitStack() as ctx:
        lists = ctx.enter_context(tc.tile_pool(name="lists", bufs=1))
        keep = ctx.enter_context(tc.tile_pool(name="keep", bufs=1))
        psum = ctx.enter_context(tc.psum_pool(name="psum", bufs=1))

        def load_list(source, name):
            tile = lists.tile([P, S // GROUP], U16, name=name)
            nc.sync.dma_start(tile[:], source)
            return tile

        def zero_bytes(tile):
            nc.vector.memset(tile[:].bitcast(I32), 0)

        def place_scale_rows(placed, picked):
            for c in range(PACK):
                nc.sync.dma_start(
                    placed[c:P:QUADRANT, :].bitcast(I32), picked[BLOCK_PARTITIONS * c : P : QUADRANT, :].bitcast(I32)
                )

        def deal_pair(dealt, picked, first):
            nc.vector.tensor_copy(
                out=dealt.rearrange("p (t m) -> p m t", t=2),
                in_=picked.rearrange("p (m t) -> p m t", t=PACK)[:, :, first : first + 2],
            )

        def by_row_tile(early_pair, late_pair):
            return [pair[:, i * P : (i + 1) * P] for pair in (early_pair, late_pair) for i in range(2)]

        def product(t, pieces, stationary, stationary_scales, moving, moving_scales):
            banks = []
            for i, cols in enumerate(pieces):
                bank = psum.tile([P, width(cols)], F32, name="bank", tag="bank%d_%d" % (t, i))
                nc.tensor.matmul_mx(
                    out=bank[:],
                    lhsT=stationary.bitcast(FP8X4),
                    lhsT_scale=stationary_scales,
                    rhs=moving[:, cols].bitcast(FP8X4),
                    rhs_scale=moving_scales[:, cols],
                    start=True,
                    stop=True,
                )
                banks.append((cols, bank))
            return banks

        def empty(target, banks, func):
            for cols, bank in banks:
                nc.scalar.activation(target[:, cols], bank[:], func, scale=SIXTEENTH)

        x_byte_table = keep.tile([P, T], U8, name="x_byte_table", align_bytes=64)
        d_byte_table = keep.tile([P, G], U8, name="d_byte_table", tag="d_bytes_then_tokens", align_bytes=64)
        zero_bytes(d_byte_table)
        zero_bytes(x_byte_table)

        k1_list = load_list(k1, "k1_list")
        offs_list = load_list(offs, "offs_list")
        nc.sync.dma_start(d_byte_table[0:P:BLOCK_PARTITIONS, :].bitcast(I32), d_scales[0].bitcast(I32))
        nc.sync.dma_start(x_byte_table[0:P:BLOCK_PARTITIONS, :].bitcast(I32), x_scales[0].bitcast(I32))
        cand_list = load_list(cand, "cand_list")
        n1_list = load_list(n1, "n1_list")
        x_word_table = keep.tile([P, T], I32, name="x_word_table", align_bytes=64)
        nc.sync.dma_start(x_word_table[:], x_words[0].rearrange("p n t -> p (n t)").bitcast(I32))
        d_word_table = keep.tile([P, G], I32, name="d_word_table", align_bytes=64)
        nc.sync.dma_start(d_word_table[:], d_words[0].rearrange("p n t -> p (n t)").bitcast(I32))
        n2_list = load_list(n2, "n2_list")
        gain = keep.tile([P, PACK], F32, name="gain")
        nc.sync.dma_start(gain[:], gs.rearrange("(p t) o -> p (t o)", t=PACK))
        n4_list = load_list(n4, "n4_list")
        n3_list = load_list(n3, "n3_list")

        first_placed = keep.tile([P, H + S], U8, name="first_placed", align_bytes=64)
        cand_placed = keep.tile([P, C], U8, name="cand_placed", align_bytes=64)
        zero_bytes(first_placed)
        windows = [keep.tile([P, 2 * S], F32, name="window%d" % t) for t in range(PACK)]
        nc.vector.memset(windows[0][:, S:], 0.0)
        zero_bytes(cand_placed)
        even_page = keep.tile([P, U], F32, name="even_page")
        nc.vector.memset(even_page[:], 0.0)

        first_picked = keep.tile([P, H + S], U8, name="first_picked", tag="bytes_then_d_late", align_bytes=64)
        nc.vector.tensor_copy(first_picked[:, :H], d_byte_table[:].indirect(k1_list[:]))
        nc.vector.tensor_copy(first_picked[:, H:], x_byte_table[:].indirect(offs_list[:]))
        place_scale_rows(first_placed, first_picked)
        token_words = keep.tile([P, S], U32, name="token_words", tag="d_bytes_then_tokens", align_bytes=64)
        nc.vector.tensor_copy(token_words[:], x_word_table[:].bitcast(U32).indirect(offs_list[:]))
        d_picked = keep.tile([P, H], U32, name="d_picked", tag="d_words_then_cand_bytes", align_bytes=64)
        nc.vector.tensor_copy(d_picked[:], d_word_table[:].bitcast(U32).indirect(k1_list[:]))
        d_early = keep.tile([P, H // 2], U32, name="d_early", align_bytes=64)
        deal_pair(d_early[:], d_picked[:], 0)
        d_scale_dealt = keep.tile([P, H], U8, name="d_scale_dealt", align_bytes=64)
        deal_pair(d_scale_dealt[:, : H // 2], first_placed[:, :H], 0)
        d_late = keep.tile([P, H // 2], U32, name="d_late", tag="bytes_then_d_late", align_bytes=64)
        deal_pair(d_late[:], d_picked[:], 2)
        deal_pair(d_scale_dealt[:, H // 2 :], first_placed[:, :H], 2)
        d_tiles = by_row_tile(d_early, d_late)

        cand_bytes = keep.tile([P, C], U8, name="cand_bytes", tag="d_words_then_cand_bytes", align_bytes=64)
        nc.vector.tensor_copy(cand_bytes[:], x_byte_table[:].indirect(cand_list[:]))
        place_scale_rows(cand_placed, cand_bytes)

        for t in range(PACK):
            d_scale_tile = d_scale_dealt[:, t * P : (t + 1) * P]
            pieces = HALVES if t == 0 else WHOLE
            empty(windows[t], product(t, pieces, d_tiles[t], d_scale_tile, token_words, first_placed[:, H:]), ACT.Copy)

        z_grouped = [
            keep.tile([P, width(cols), PACK], BF16, name="z_grouped", tag="z_grouped%d" % i, align_bytes=64)
            for i, cols in enumerate(Z_PIECES)
        ]
        last_at_n1 = keep.tile([P, S], F32, name="last_at_n1", tag="n1_then_cand_then_page", align_bytes=64)
        at_n1 = [windows[t + 1][:, S:] for t in range(LAST)] + [last_at_n1[:]]
        at_n2 = [keep.tile([P, S], F32, name="at_n2_%d" % t) for t in range(PACK)]
        larger = [keep.tile([P, S], F32, name="larger", tag="larger%d" % t, align_bytes=64) for t in range(PACK)]
        smaller = [keep.tile([P, S], F32, name="smaller", tag="smaller%d" % t, align_bytes=64) for t in range(PACK)]

        def finish_z(t):
            for cols in HALVES if t == LAST else WHOLE:
                nc.vector.tensor_tensor(smaller[t][:, cols], larger[t][:, cols], at_n2[t][:, cols], ALU.min)
            for i, cols in enumerate(Z_PIECES):
                nc.scalar.activation(z_grouped[i][:, :, t], smaller[t][:, cols], ACT.Copy, scale=gain[:, t : t + 1])

        for t in range(PACK):
            nc.vector.tensor_copy(at_n1[t], windows[t][:].indirect(n1_list[:]))
            if t > 0:
                finish_z(t - 1)
            nc.vector.tensor_copy(at_n2[t][:], windows[t][:].indirect(n2_list[:]))
            nc.vector.tensor_tensor(larger[t][:], windows[t][:, :S], at_n1[t], ALU.max)
        finish_z(LAST)

        cand_picked = keep.tile([P, C], U32, name="cand_picked", tag="n1_then_cand_then_page", align_bytes=64)
        nc.vector.tensor_copy(cand_picked[:], x_word_table[:].bitcast(U32).indirect(cand_list[:]))
        cand_scale_early = keep.tile([P, C // 2], U8, name="cand_scale_early", tag="larger%d" % LAST, align_bytes=64)
        deal_pair(cand_scale_early[:], cand_placed[:], 0)
        cand_early = keep.tile([P, C // 2], U32, name="cand_early", align_bytes=64)
        deal_pair(cand_early[:], cand_picked[:], 0)

        z_words = keep.tile([P, S], U32, name="z_words", align_bytes=64)
        z_scales = keep.tile([P, S], U8, name="z_scales", align_bytes=64)
        for i, cols in enumerate(Z_PIECES):
            nc.vector.quantize_mx(
                out=z_words[:, cols].bitcast(FP8X4),
                scales=z_scales[:, cols],
                in_=z_grouped[i][:].rearrange("p s t -> p (s t)"),
            )

        cand_scale_late = keep.tile([P, C // 2], U8, name="cand_scale_late", tag="smaller%d" % LAST, align_bytes=64)
        deal_pair(cand_scale_late[:], cand_placed[:], 2)
        last_z_tag = "z_grouped%d" % (len(Z_PIECES) - 1)
        cand_late = keep.tile([P, C // 2], U32, name="cand_late", tag=last_z_tag, align_bytes=64)
        deal_pair(cand_late[:], cand_picked[:], 2)
        cand_tiles = by_row_tile(cand_early, cand_late)
        cand_scale_tiles = by_row_tile(cand_scale_early, cand_scale_late)

        odd_page = keep.tile([P, U], F32, name="odd_page", tag="n1_then_cand_then_page", align_bytes=64)
        nc.vector.memset(odd_page[:], 0.0)
        pages = [even_page, odd_page]

        scores = [keep.tile([P, S], F32, name="score%d" % t) for t in range(PACK)]
        s_banks = []
        for t in range(PACK):
            pieces = Z_PIECES if t == 0 else WHOLE
            s_banks.append(product(t, pieces, cand_tiles[t], cand_scale_tiles[t], z_words, z_scales))
            empty(windows[t], s_banks[t], ACT.Relu)
            if t > 0:
                empty(scores[t - 1], s_banks[t - 1], ACT.Copy)
        empty(scores[LAST], s_banks[LAST], ACT.Copy)

        out_grouped = [
            keep.tile([P, width(cols), PACK], BF16, name="out_grouped%d" % i, align_bytes=64)
            for i, cols in enumerate(PAGE_PIECES)
        ]
        out_words = keep.tile([P, U], U32, name="out_words", align_bytes=64)
        out_scales = keep.tile([P, U], U8, name="out_scales", align_bytes=64)
        out_rows = out_0.rearrange("(p t) u -> t p u", t=PACK)
        negated = [keep.tile([P, S], F32, name="negated%d" % t) for t in range(PACK)]

        def look_up(t):
            nc.vector.tensor_scalar(negated[t][:], windows[t][:].indirect(n4_list[:]), -1.0, 0.0, ALU.mult, ALU.add)

        look_up(0)
        for t in range(PACK):
            if t < LAST:
                look_up(t + 1)
            page = pages[t % len(pages)]
            nc.vector.tensor_tensor(page[:].indirect(n3_list[:]), scores[t][:], negated[t][:], ALU.add)
            nc.sync.dma_start(out_rows[t], page[:])
            for i, cols in enumerate(PAGE_PIECES):
                if cols == VECTOR_PIECE and t == LAST - 1:
                    twice = page[:, cols].unsqueeze(2).broadcast_to([P, width(cols), 2])
                    nc.scalar.copy(out_grouped[i][:, :, t:], twice)
                elif cols == VECTOR_PIECE and t == LAST:
                    nc.vector.tensor_copy(out_grouped[i][:, :, t], page[:, cols])
                else:
                    nc.scalar.copy(out_grouped[i][:, :, t], page[:, cols])

        out_word_rows = out_1[0].rearrange("p u t -> p (u t)").bitcast(I32)
        for i, cols in enumerate(PAGE_PIECES):
            nc.vector.quantize_mx(
                out=out_words[:, cols].bitcast(FP8X4),
                scales=out_scales[:, cols],
                in_=out_grouped[i][:].rearrange("p u t -> p (u t)"),
            )
            nc.sync.dma_start(out_word_rows[:, cols], out_words[:, cols].bitcast(I32))
        for q in range(P // QUADRANT):
            queue = nc.scalar if q % 2 == 0 else nc.sync
            queue.dma_start(
                out_2[0, PACK * q : PACK * (q + 1), :].bitcast(I32),
                out_scales[QUADRANT * q : QUADRANT * q + PACK, :].bitcast(I32),
            )
